import numpy as np, ml_dtypes
CORES = [44,45,46,47,172,173,174,175,300,301,302,303,428,429,430,431]
N = 16
QP = 32
def setup_inputs(rng):
    m = 150 * rng.standard_normal((1, QP, 1), dtype=np.float32) + 3 * rng.standard_normal((N, QP, 1), dtype=np.float32)
    m = (m + rng.uniform(100, 300, (1, QP, 1)) * (rng.random((1, QP, 1)) < 0.7) * (rng.random((N, QP, 1)) < 0.5)).astype(np.float32)
    l = 20 * (1 + np.abs(rng.standard_normal((N, QP, 1), dtype=np.float32)))
    return {"o": (l * rng.standard_normal((N, QP, 128), dtype=np.float32) / 4).astype(ml_dtypes.bfloat16), "ml": np.concatenate([m, l], axis=2)}
def setup_inputs_big(rng):
    d = setup_inputs(rng)
    for k in ("o",): d[k] = (d[k].astype(np.float32) * 1048576.0).astype(d[k].dtype)
    return d
def setup_inputs_small(rng):
    d = setup_inputs(rng)
    for k in ("o",): d[k] = (d[k].astype(np.float32) * (1 / 1048576.0)).astype(d[k].dtype)
    return d
def setup_inputs_apart(rng):
    d = setup_inputs(rng)
    f = (10.0 ** rng.permutation(np.linspace(-1.5, 1.5, N))).astype(np.float32).reshape(N, 1, 1)
    for k in ("o",): d[k] = (d[k].astype(np.float32) * f).astype(d[k].dtype)
    return d
def reference(o, ml):
    O, ML = o.astype(np.float64), ml.astype(np.float64)
    m, l = ML[:, :, 0:1], ML[:, :, 1:2]
    f = np.exp(m - m.max(axis=0))
    y = ((f * O).sum(axis=0) / (f * l).sum(axis=0)).astype(ml_dtypes.bfloat16)
    return {"y": np.broadcast_to(y, (N,) + y.shape)}

@@ -1,0 +1,153 @@
+from concourse.bass import DstId, RemoteDMATransfer
+from concourse.mybir import AluOpType, AxisListType, ActivationFunctionType
+
+W = 40
+ENG = 4
+NQ = 32
+
+SCRATCH = {
+    "L1": ("sbuf", [128, 4 * W], "bfloat16"),
+    "L2": ("sbuf", [128, 4 * W], "bfloat16"),
+    "ramp1": ("sbuf", [128, 128], "float32"),
+    "ramp2": ("sbuf", [128, 128], "float32"),
+    "rep": ("sbuf", [128, 128], "bfloat16"),
+    "ident": ("sbuf", [128, 128], "bfloat16"),
+    "mlsb": ("sbuf", [128, 2], "float32"),
+    "meta": ("sbuf", [128, 8], "bfloat16"),
+    "psa": ("psum", [128, 8], "float32"),
+    "psb": ("psum", [128, 32], "float32"),
+    "e0": ("sbuf", [128, 4], "float32"),
+    "ownp": ("sbuf", [128, 36], "float32"),
+    "m4": ("sbuf", [128, 4], "float32"),
+    "f4": ("sbuf", [128, 4], "float32"),
+    "pr": ("sbuf", [128, 4 * 36], "float32"),
+    "sm": ("sbuf", [128, 2 * 36], "float32"),
+    "nrm": ("sbuf", [128, 4], "float32"),
+    "w4": ("sbuf", [128, 4], "float32"),
+    "wl": ("sbuf", [128, 4], "float32"),
+    "den": ("sbuf", [128, 4], "float32"),
+    "rc": ("sbuf", [128, 4], "float32"),
+    "q": ("sbuf", [128, 4 * 32], "bfloat16"),
+    "ysb": ("sbuf", [128, 32], "bfloat16"),
+}
+SEMAPHORES = ["ld_o", "ld_ml", "ramp1", "ramp2", "rep", "ident", "hi", "mid", "mm", "pay1", "e0", "own", "m40", "a1",
+              "sent", "negr", "m4", "f4", "p0", "p1", "p2", "p3", "s1", "s2", "pay2", "a2", "nrm", "w4", "wl", "den",
+              "rc", "q0", "q1", "q2", "q3", "acc", "y", "st"]
+
+
+def rank_program(g, core, T, topo):
+    if T.rank_of(core) is None:
+        return
+    V, A, PE, SY, S = g.vector, g.scalar, g.tensor, g.sync, T.sem
+    ADD, SUB, MUL = AluOpType.add, AluOpType.subtract, AluOpType.mult
+    EXP, COPY = ActivationFunctionType.Exp, ActivationFunctionType.Copy
+    L1, L2 = T.L1, T.L2
+
+    ranks = list(T.cores)
+    here = [c for c in ranks if topo.host(c) == topo.host(core) and topo.chip(c) == topo.chip(core)]
+    plane = [c for c in ranks if topo.same_plane(core, c)]
+    cable = [c for c in ranks if topo.rack(topo.host(c)) != topo.rack(topo.host(core)) and topo.may_write(core, c)]
+    k = here.index(core)
+    far1, far2 = (plane, cable) if k % 2 == 0 else (cable, plane)
+
+    def send(buf, c0, c1, dests, rsem):
+        taken, trs = [], []
+        for d, slot in sorted(dests, key=lambda x: topo.mask(core, x[0])):
+            m = topo.mask(core, d)
+            eng = [e for e in range(m.bit_length()) if (m >> e) & 1 and e not in taken][:ENG]
+            taken.extend(eng)
+            rid, pid = topo.addr(d, core)
+            trs.append(RemoteDMATransfer(dst_ids=[DstId(rid=rid, pnc=pid)], dma_engine_mask=sum(1 << e for e in eng),
+                                         remote_sem=rsem, src=buf[:, c0:c1], dst=buf[:, slot * W + c0:slot * W + c1]))
+        g.remote_dma_fused(trs, local_sem=S.sent)
+
+    A.dma_start(T.mlsb[0:NQ, :], T.ml[:, :]).then_inc(S.ld_ml, 16)
+    SY.dma_start(L1[:, 8:40], T.o[:, :]).then_inc(S.ld_o, 16)
+    g.iota(T.ramp1[0:NQ, :], [[1, NQ], [0, 4]], 0, -1, allow_small_or_imprecise_dtypes=True).then_inc(S.ramp1, 1)
+    V.wait_ge(S.ramp1, 1)
+    V.tensor_scalar(T.rep[0:NQ, :], T.ramp1[0:NQ, :], 0.0, None, AluOpType.is_equal).then_inc(S.rep, 1)
+    V.wait_ge(S.ld_ml, 16)
+    V.tensor_copy(T.meta[0:NQ, 1:3], T.mlsb[0:NQ, 0:2]).then_inc(S.hi, 1)
+    V.wait_ge(S.hi, 1)
+    V.tensor_tensor(T.meta[0:NQ, 0:1], T.mlsb[0:NQ, 0:1], T.meta[0:NQ, 1:2], SUB).then_inc(S.mid, 1)
+    PE.wait_ge(S.rep, 1)
+    PE.wait_ge(S.hi, 1)
+    PE.wait_ge(S.mid, 1)
+    PE.matmul(T.psa[:, 0:3], T.rep[0:NQ, :], T.meta[0:NQ, 0:3], True, True).then_inc(S.mm, 1)
+    V.wait_ge(S.mm, 1)
+    V.tensor_copy(L1[:, 5:8], T.psa[:, 0:3]).then_inc(S.pay1, 1)
+
+    g.wait_ge(S.ld_o, 16)
+    g.wait_ge(S.pay1, 1)
+    send(L1, 5, 40, [(here[k ^ 2], 1), (far1[k], 2), (far1[k ^ 2], 3)], S.a1)
+    g.iota(T.ramp2[:, :], [[-1, 128]], 0, 1, allow_small_or_imprecise_dtypes=True).then_inc(S.ramp2, 1)
+
+    A.wait_ge(S.pay1, 1)
+    A.activation(T.e0[:, 0:1], L1[:, 5:6], EXP).then_inc(S.e0, 1)
+    A.wait_ge(S.e0, 1)
+    A.wait_ge(S.ld_o, 16)
+    A.activation(T.ownp[:, 0:33], L1[:, 7:40], COPY, scale=T.e0[:, 0:1]).then_inc(S.own, 1)
+    V.wait_ge(S.pay1, 1)
+    V.tensor_copy(T.m4[:, 0:1], L1[:, 6:7]).then_inc(S.m40, 1)
+
+    V.wait_ge(S.a1, 3 * ENG)
+    V.tensor_reduce(L2[:, 6:7], L1[:, 6:4 * W:W], AxisListType.X, AluOpType.max, negate=True).then_inc(S.negr, 1)
+    V.tensor_tensor(T.m4[:, 1:4], L1[:, W + 6:4 * W:W], L1[:, W + 5:4 * W:W], ADD).then_inc(S.m4, 1)
+    A.wait_ge(S.a1, 3 * ENG)
+    A.wait_ge(S.m40, 1)
+    A.wait_ge(S.negr, 1)
+    A.wait_ge(S.m4, 1)
+    A.activation(T.f4[:, 0:4], T.m4[:, 0:4], EXP, bias=L2[:, 6:7]).then_inc(S.f4, 1)
+    A.wait_ge(S.f4, 1)
+    for j in (1, 2, 3):
+        A.activation(T.pr[:, 36 * j:36 * j + 33], L1[:, W * j + 7:W * j + 40], COPY,
+                     scale=T.f4[:, j:j + 1]).then_inc(S["p%d" % j], 1)
+    V.wait_ge(S.f4, 1)
+    V.wait_ge(S.own, 1)
+    V.tensor_scalar(T.pr[:, 0:33], T.ownp[:, 0:33], T.f4[:, 0:1], None, MUL).then_inc(S.p0, 1)
+    V.wait_ge(S.p0, 1)
+    V.wait_ge(S.p1, 1)
+    V.tensor_tensor(T.sm[:, 0:33], T.pr[:, 0:33], T.pr[:, 36:69], ADD).then_inc(S.s1, 1)
+    V.wait_ge(S.s1, 1)
+    V.wait_ge(S.p2, 1)
+    V.tensor_tensor(T.sm[:, 36:69], T.sm[:, 0:33], T.pr[:, 72:105], ADD).then_inc(S.s2, 1)
+    V.wait_ge(S.s2, 1)
+    V.wait_ge(S.p3, 1)
+    V.tensor_tensor(L2[:, 7:40], T.sm[:, 36:69], T.pr[:, 108:141], ADD).then_inc(S.pay2, 1)
+
+    g.wait_ge(S.negr, 1)
+    g.wait_ge(S.pay2, 1)
+    send(L2, 6, 40, [(here[k ^ 1], 1), (far2[k], 2), (far2[k ^ 1], 3)], S.a2)
+
+    V.wait_ge(S.ramp2, 1)
+    V.tensor_scalar(T.ident[:, :], T.ramp2[:, :], 0.0, None, AluOpType.is_equal).then_inc(S.ident, 1)
+
+    V.wait_ge(S.pay2, 1)
+    V.wait_ge(S.a2, 3 * ENG)
+    V.tensor_reduce(T.nrm[:, 0:1], L2[:, 6:4 * W:W], AxisListType.X, AluOpType.min).then_inc(S.nrm, 1)
+    A.wait_ge(S.pay2, 1)
+    A.wait_ge(S.a2, 3 * ENG)
+    A.wait_ge(S.nrm, 1)
+    A.activation(T.w4[:, 0:4], L2[:, 6:4 * W:W], EXP, bias=T.nrm[:, 0:1], scale=-1.0).then_inc(S.w4, 1)
+    A.wait_ge(S.w4, 1)
+    PE.wait_ge(S.ident, 1)
+    for j in range(4):
+        A.activation(T.q[:, 32 * j:32 * j + 32], L2[:, W * j + 8:W * j + 40], COPY,
+                     scale=T.w4[:, j:j + 1]).then_inc(S["q%d" % j], 1)
+        PE.wait_ge(S["q%d" % j], 1)
+        mm = PE.matmul(T.psb[:, 0:32], T.ident[:, :], T.q[:, 32 * j:32 * j + 32], j == 0, j == 3)
+    mm.then_inc(S.acc, 1)
+    V.wait_ge(S.w4, 1)
+    V.tensor_tensor(T.wl[:, 0:4], T.w4[:, 0:4], L2[:, 7:4 * W:W], MUL).then_inc(S.wl, 1)
+    V.wait_ge(S.wl, 1)
+    V.tensor_reduce(T.den[:, 0:1], T.wl[:, 0:4], AxisListType.X, ADD).then_inc(S.den, 1)
+    V.wait_ge(S.den, 1)
+    V.reciprocal(T.rc[:, 0:1], T.den[:, 0:1]).then_inc(S.rc, 1)
+    V.wait_ge(S.rc, 1)
+    V.wait_ge(S.acc, 1)
+    V.tensor_scalar(T.ysb[:, :], T.psb[:, 0:32], T.rc[:, 0:1], None, MUL).then_inc(S.y, 1)
+
+    SY.wait_ge(S.y, 1)
+    SY.dma_start(T.y[:, :], T.ysb[:, :]).then_inc(S.st, 16)
+    SY.wait_ge(S.st, 16)
+    g.wait_ge(S.sent, 6 * ENG)

@@ -4,17 +4,15 @@ from concourse.mybir import AluOpType, AxisListType, ActivationFunctionType
 W = 40
 ENG = 4
 NQ = 32
+CB = 4
+CRND = 100663296.0
 
 SCRATCH = {
     "L1": ("sbuf", [128, 4 * W], "bfloat16"),
     "L2": ("sbuf", [128, 4 * W], "bfloat16"),
-    "ramp1": ("sbuf", [128, 128], "float32"),
     "ramp2": ("sbuf", [128, 128], "float32"),
-    "rep": ("sbuf", [128, 128], "bfloat16"),
     "ident": ("sbuf", [128, 128], "bfloat16"),
-    "mlsb": ("sbuf", [128, 2], "float32"),
-    "meta": ("sbuf", [128, 8], "bfloat16"),
-    "psa": ("psum", [128, 8], "float32"),
+    "mlb": ("sbuf", [128, 12], "float32"),
     "psb": ("psum", [128, 32], "float32"),
     "e0": ("sbuf", [128, 4], "float32"),
     "ownp": ("sbuf", [128, 36], "float32"),
@@ -30,7 +28,7 @@ SCRATCH = {
     "q": ("sbuf", [128, 4 * 32], "bfloat16"),
     "ysb": ("sbuf", [128, 32], "bfloat16"),
 }
-SEMAPHORES = ["ld_o", "ld_ml", "ramp1", "ramp2", "rep", "ident", "hi", "mid", "mm", "pay1", "e0", "own", "m40", "a1",
+SEMAPHORES = ["ld_o", "ld_ml", "cst", "ramp2", "ident", "pay1", "lcp", "e0", "own", "m40", "a1",
               "sent", "negr", "m4", "f4", "p0", "p1", "p2", "p3", "s1", "s2", "pay2", "a2", "nrm", "w4", "wl", "den",
               "rc", "q0", "q1", "q2", "q3", "acc", "y", "st"]
 
@@ -41,7 +39,7 @@ def rank_program(g, core, T, topo):
     V, A, PE, SY, S = g.vector, g.scalar, g.tensor, g.sync, T.sem
     ADD, SUB, MUL = AluOpType.add, AluOpType.subtract, AluOpType.mult
     EXP, COPY = ActivationFunctionType.Exp, ActivationFunctionType.Copy
-    L1, L2 = T.L1, T.L2
+    L1, L2, MLB = T.L1, T.L2, T.mlb
 
     ranks = list(T.cores)
     here = [c for c in ranks if topo.host(c) == topo.host(core) and topo.chip(c) == topo.chip(core)]
@@ -61,38 +59,35 @@ def rank_program(g, core, T, topo):
                                          remote_sem=rsem, src=buf[:, c0:c1], dst=buf[:, slot * W + c0:slot * W + c1]))
         g.remote_dma_fused(trs, local_sem=S.sent)
 
-    A.dma_start(T.mlsb[0:NQ, :], T.ml[:, :]).then_inc(S.ld_ml, 16)
+    for cb in range(CB):
+        (SY if cb < CB // 2 else A).dma_start(MLB[cb:128:CB, 4:6], T.ml[:, :]).then_inc(S.ld_ml, 16)
     SY.dma_start(L1[:, 8:40], T.o[:, :]).then_inc(S.ld_o, 16)
-    g.iota(T.ramp1[0:NQ, :], [[1, NQ], [0, 4]], 0, -1, allow_small_or_imprecise_dtypes=True).then_inc(S.ramp1, 1)
-    V.wait_ge(S.ramp1, 1)
-    V.tensor_scalar(T.rep[0:NQ, :], T.ramp1[0:NQ, :], 0.0, None, AluOpType.is_equal).then_inc(S.rep, 1)
-    V.wait_ge(S.ld_ml, 16)
-    V.tensor_copy(T.meta[0:NQ, 1:3], T.mlsb[0:NQ, 0:2]).then_inc(S.hi, 1)
-    V.wait_ge(S.hi, 1)
-    V.tensor_tensor(T.meta[0:NQ, 0:1], T.mlsb[0:NQ, 0:1], T.meta[0:NQ, 1:2], SUB).then_inc(S.mid, 1)
-    PE.wait_ge(S.rep, 1)
-    PE.wait_ge(S.hi, 1)
-    PE.wait_ge(S.mid, 1)
-    PE.matmul(T.psa[:, 0:3], T.rep[0:NQ, :], T.meta[0:NQ, 0:3], True, True).then_inc(S.mm, 1)
-    V.wait_ge(S.mm, 1)
-    V.tensor_copy(L1[:, 5:8], T.psa[:, 0:3]).then_inc(S.pay1, 1)
+    V.memset(MLB[:, 0:1], CRND).then_inc(S.cst, 1)
+    V.memset(MLB[:, 8:9], 0.0).then_inc(S.cst, 1)
+    V.wait_ge(S.cst, 2)
+    V.wait_ge(S.ld_ml, 16 * CB)
+    V.tensor_tensor_scan(L1[:, 5:7], MLB[:, 4:12:4], MLB[:, 0:8:4], CRND, ADD, SUB).then_inc(S.pay1, 1)
+    A.wait_ge(S.ld_ml, 16 * CB)
+    A.activation(L1[:, 7:8], MLB[:, 5:6], COPY).then_inc(S.lcp, 1)
 
     g.wait_ge(S.ld_o, 16)
+    g.wait_ge(S.lcp, 1)
     g.wait_ge(S.pay1, 1)
     send(L1, 5, 40, [(here[k ^ 2], 1), (far1[k], 2), (far1[k ^ 2], 3)], S.a1)
     g.iota(T.ramp2[:, :], [[-1, 128]], 0, 1, allow_small_or_imprecise_dtypes=True).then_inc(S.ramp2, 1)
 
     A.wait_ge(S.pay1, 1)
-    A.activation(T.e0[:, 0:1], L1[:, 5:6], EXP).then_inc(S.e0, 1)
+    A.activation(T.e0[:, 0:1], L1[:, 6:7], EXP, scale=-1.0).then_inc(S.e0, 1)
     A.wait_ge(S.e0, 1)
+    A.wait_ge(S.lcp, 1)
     A.wait_ge(S.ld_o, 16)
     A.activation(T.ownp[:, 0:33], L1[:, 7:40], COPY, scale=T.e0[:, 0:1]).then_inc(S.own, 1)
     V.wait_ge(S.pay1, 1)
-    V.tensor_copy(T.m4[:, 0:1], L1[:, 6:7]).then_inc(S.m40, 1)
+    V.tensor_copy(T.m4[:, 0:1], L1[:, 5:6]).then_inc(S.m40, 1)
 
     V.wait_ge(S.a1, 3 * ENG)
-    V.tensor_reduce(L2[:, 6:7], L1[:, 6:4 * W:W], AxisListType.X, AluOpType.max, negate=True).then_inc(S.negr, 1)
-    V.tensor_tensor(T.m4[:, 1:4], L1[:, W + 6:4 * W:W], L1[:, W + 5:4 * W:W], ADD).then_inc(S.m4, 1)
+    V.tensor_reduce(L2[:, 6:7], L1[:, 5:4 * W:W], AxisListType.X, AluOpType.max, negate=True).then_inc(S.negr, 1)
+    V.tensor_tensor(T.m4[:, 1:4], L1[:, W + 5:4 * W:W], L1[:, W + 6:4 * W:W], SUB).then_inc(S.m4, 1)
     A.wait_ge(S.a1, 3 * ENG)
     A.wait_ge(S.m40, 1)
     A.wait_ge(S.negr, 1)

@@ -2,6 +2,7 @@ from concourse.bass import DstId, RemoteDMATransfer
 from concourse.mybir import AluOpType, AxisListType, ActivationFunctionType
 
 W = 40
+WR = 8
 ENG = 4
 NQ = 32
 CB = 4
@@ -10,10 +11,12 @@ CRND = 100663296.0
 SCRATCH = {
     "L1": ("sbuf", [128, 4 * W], "bfloat16"),
     "L2": ("sbuf", [128, 4 * W], "bfloat16"),
+    "NR": ("sbuf", [128, 4 * WR], "bfloat16"),
     "ramp2": ("sbuf", [128, 128], "float32"),
     "ident": ("sbuf", [128, 128], "bfloat16"),
+    "dg": ("sbuf", [128, 4 * 128], "bfloat16"),
     "mlb": ("sbuf", [128, 12], "float32"),
-    "psb": ("psum", [128, 32], "float32"),
+    "psb": ("psum", [128, 40], "float32"),
     "e0": ("sbuf", [128, 4], "float32"),
     "ownp": ("sbuf", [128, 36], "float32"),
     "m4": ("sbuf", [128, 4], "float32"),
@@ -22,15 +25,12 @@ SCRATCH = {
     "sm": ("sbuf", [128, 2 * 36], "float32"),
     "nrm": ("sbuf", [128, 4], "float32"),
     "w4": ("sbuf", [128, 4], "float32"),
-    "wl": ("sbuf", [128, 4], "float32"),
-    "den": ("sbuf", [128, 4], "float32"),
     "rc": ("sbuf", [128, 4], "float32"),
-    "q": ("sbuf", [128, 4 * 32], "bfloat16"),
     "ysb": ("sbuf", [128, 32], "bfloat16"),
 }
 SEMAPHORES = ["ld_o", "ld_ml", "cst", "ramp2", "ident", "pay1", "lcp", "e0", "own", "m40", "a1",
-              "sent", "negr", "m4", "f4", "p0", "p1", "p2", "p3", "s1", "s2", "pay2", "a2", "nrm", "w4", "wl", "den",
-              "rc", "q0", "q1", "q2", "q3", "acc", "y", "st"]
+              "sent", "negr", "m4", "f4", "p0", "p1", "p2", "p3", "s1", "s2", "pay2", "ar", "a2", "nrm", "w4",
+              "rc", "d0", "d1", "d2", "d3", "acc", "y", "st"]
 
 
 def rank_program(g, core, T, topo):
@@ -39,7 +39,7 @@ def rank_program(g, core, T, topo):
     V, A, PE, SY, S = g.vector, g.scalar, g.tensor, g.sync, T.sem
     ADD, SUB, MUL = AluOpType.add, AluOpType.subtract, AluOpType.mult
     EXP, COPY = ActivationFunctionType.Exp, ActivationFunctionType.Copy
-    L1, L2, MLB = T.L1, T.L2, T.mlb
+    L1, L2, NR, MLB = T.L1, T.L2, T.NR, T.mlb
 
     ranks = list(T.cores)
     here = [c for c in ranks if topo.host(c) == topo.host(core) and topo.chip(c) == topo.chip(core)]
@@ -48,7 +48,7 @@ def rank_program(g, core, T, topo):
     k = here.index(core)
     far1, far2 = (plane, cable) if k % 2 == 0 else (cable, plane)
 
-    def send(buf, c0, c1, dests, rsem):
+    def send(buf, w, c0, c1, dests, rsem):
         taken, trs = [], []
         for d, slot in sorted(dests, key=lambda x: topo.mask(core, x[0])):
             m = topo.mask(core, d)
@@ -56,7 +56,7 @@ def rank_program(g, core, T, topo):
             taken.extend(eng)
             rid, pid = topo.addr(d, core)
             trs.append(RemoteDMATransfer(dst_ids=[DstId(rid=rid, pnc=pid)], dma_engine_mask=sum(1 << e for e in eng),
-                                         remote_sem=rsem, src=buf[:, c0:c1], dst=buf[:, slot * W + c0:slot * W + c1]))
+                                         remote_sem=rsem, src=buf[:, c0:c1], dst=buf[:, slot * w + c0:slot * w + c1]))
         g.remote_dma_fused(trs, local_sem=S.sent)
 
     for cb in range(CB):
@@ -73,7 +73,7 @@ def rank_program(g, core, T, topo):
     g.wait_ge(S.ld_o, 16)
     g.wait_ge(S.lcp, 1)
     g.wait_ge(S.pay1, 1)
-    send(L1, 5, 40, [(here[k ^ 2], 1), (far1[k], 2), (far1[k ^ 2], 3)], S.a1)
+    send(L1, W, 5, 40, [(here[k ^ 2], 1), (far1[k], 2), (far1[k ^ 2], 3)], S.a1)
     g.iota(T.ramp2[:, :], [[-1, 128]], 0, 1, allow_small_or_imprecise_dtypes=True).then_inc(S.ramp2, 1)
 
     A.wait_ge(S.pay1, 1)
@@ -84,15 +84,22 @@ def rank_program(g, core, T, topo):
     A.activation(T.ownp[:, 0:33], L1[:, 7:40], COPY, scale=T.e0[:, 0:1]).then_inc(S.own, 1)
     V.wait_ge(S.pay1, 1)
     V.tensor_copy(T.m4[:, 0:1], L1[:, 5:6]).then_inc(S.m40, 1)
+    V.wait_ge(S.ramp2, 1)
+    V.tensor_scalar(T.ident[:, :], T.ramp2[:, :], 0.0, None, AluOpType.is_equal).then_inc(S.ident, 1)
 
     V.wait_ge(S.a1, 3 * ENG)
-    V.tensor_reduce(L2[:, 6:7], L1[:, 5:4 * W:W], AxisListType.X, AluOpType.max, negate=True).then_inc(S.negr, 1)
+    V.tensor_reduce(NR[:, 0:1], L1[:, 5:4 * W:W], AxisListType.X, AluOpType.max, negate=True).then_inc(S.negr, 1)
     V.tensor_tensor(T.m4[:, 1:4], L1[:, W + 5:4 * W:W], L1[:, W + 6:4 * W:W], SUB).then_inc(S.m4, 1)
+
+    to2 = [(here[k ^ 1], 1), (far2[k], 2), (far2[k ^ 1], 3)]
+    g.wait_ge(S.negr, 1)
+    send(NR, WR, 0, 1, to2, S.ar)
+
     A.wait_ge(S.a1, 3 * ENG)
     A.wait_ge(S.m40, 1)
     A.wait_ge(S.negr, 1)
     A.wait_ge(S.m4, 1)
-    A.activation(T.f4[:, 0:4], T.m4[:, 0:4], EXP, bias=L2[:, 6:7]).then_inc(S.f4, 1)
+    A.activation(T.f4[:, 0:4], T.m4[:, 0:4], EXP, bias=NR[:, 0:1]).then_inc(S.f4, 1)
     A.wait_ge(S.f4, 1)
     for j in (1, 2, 3):
         A.activation(T.pr[:, 36 * j:36 * j + 33], L1[:, W * j + 7:W * j + 40], COPY,
@@ -110,39 +117,37 @@ def rank_program(g, core, T, topo):
     V.wait_ge(S.p3, 1)
     V.tensor_tensor(L2[:, 7:40], T.sm[:, 36:69], T.pr[:, 108:141], ADD).then_inc(S.pay2, 1)
 
-    g.wait_ge(S.negr, 1)
     g.wait_ge(S.pay2, 1)
-    send(L2, 6, 40, [(here[k ^ 1], 1), (far2[k], 2), (far2[k ^ 1], 3)], S.a2)
+    send(L2, W, 7, 40, to2, S.a2)
 
-    V.wait_ge(S.ramp2, 1)
-    V.tensor_scalar(T.ident[:, :], T.ramp2[:, :], 0.0, None, AluOpType.is_equal).then_inc(S.ident, 1)
-
-    V.wait_ge(S.pay2, 1)
-    V.wait_ge(S.a2, 3 * ENG)
-    V.tensor_reduce(T.nrm[:, 0:1], L2[:, 6:4 * W:W], AxisListType.X, AluOpType.min).then_inc(S.nrm, 1)
-    A.wait_ge(S.pay2, 1)
-    A.wait_ge(S.a2, 3 * ENG)
+    V.wait_ge(S.negr, 1)
+    V.wait_ge(S.ar, 3 * ENG)
+    V.tensor_reduce(T.nrm[:, 0:1], NR[:, 0:4 * WR:WR], AxisListType.X, AluOpType.min).then_inc(S.nrm, 1)
+    A.wait_ge(S.ar, 3 * ENG)
     A.wait_ge(S.nrm, 1)
-    A.activation(T.w4[:, 0:4], L2[:, 6:4 * W:W], EXP, bias=T.nrm[:, 0:1], scale=-1.0).then_inc(S.w4, 1)
+    A.activation(T.w4[:, 0:4], NR[:, 0:4 * WR:WR], EXP, bias=T.nrm[:, 0:1], scale=-1.0).then_inc(S.w4, 1)
     A.wait_ge(S.w4, 1)
-    PE.wait_ge(S.ident, 1)
-    for j in range(4):
-        A.activation(T.q[:, 32 * j:32 * j + 32], L2[:, W * j + 8:W * j + 40], COPY,
-                     scale=T.w4[:, j:j + 1]).then_inc(S["q%d" % j], 1)
-        PE.wait_ge(S["q%d" % j], 1)
-        mm = PE.matmul(T.psb[:, 0:32], T.ident[:, :], T.q[:, 32 * j:32 * j + 32], j == 0, j == 3)
-    mm.then_inc(S.acc, 1)
+    A.wait_ge(S.ident, 1)
+    A.activation(T.dg[:, 3 * 128:4 * 128], T.ident[:, :], COPY, scale=T.w4[:, 3:4]).then_inc(S.d3, 1)
     V.wait_ge(S.w4, 1)
-    V.tensor_tensor(T.wl[:, 0:4], T.w4[:, 0:4], L2[:, 7:4 * W:W], MUL).then_inc(S.wl, 1)
-    V.wait_ge(S.wl, 1)
-    V.tensor_reduce(T.den[:, 0:1], T.wl[:, 0:4], AxisListType.X, ADD).then_inc(S.den, 1)
-    V.wait_ge(S.den, 1)
-    V.reciprocal(T.rc[:, 0:1], T.den[:, 0:1]).then_inc(S.rc, 1)
-    V.wait_ge(S.rc, 1)
+    V.wait_ge(S.ident, 1)
+    for j in (0, 1, 2):
+        V.tensor_scalar(T.dg[:, j * 128:(j + 1) * 128], T.ident[:, :], T.w4[:, j:j + 1], None,
+                        MUL).then_inc(S["d%d" % j], 1)
+
+    PE.wait_ge(S.pay2, 1)
+    for j in range(4):
+        PE.wait_ge(S["d%d" % j], 1)
+        if j == 1:
+            PE.wait_ge(S.a2, 3 * ENG)
+        mm = PE.matmul(T.psb[:, 0:33], T.dg[:, j * 128:(j + 1) * 128], L2[:, W * j + 7:W * j + 40], j == 0, j == 3)
+    mm.then_inc(S.acc, 1)
     V.wait_ge(S.acc, 1)
-    V.tensor_scalar(T.ysb[:, :], T.psb[:, 0:32], T.rc[:, 0:1], None, MUL).then_inc(S.y, 1)
+    V.reciprocal(T.rc[:, 0:1], T.psb[:, 0:1]).then_inc(S.rc, 1)
+    V.wait_ge(S.rc, 1)
+    V.tensor_scalar(T.ysb[:, :], T.psb[:, 1:33], T.rc[:, 0:1], None, MUL).then_inc(S.y, 1)
 
     SY.wait_ge(S.y, 1)
     SY.dma_start(T.y[:, :], T.ysb[:, :]).then_inc(S.st, 16)
     SY.wait_ge(S.st, 16)
-    g.wait_ge(S.sent, 6 * ENG)
+    g.wait_ge(S.sent, 9 * ENG)

@@ -2,34 +2,34 @@ from concourse.bass import DstId, RemoteDMATransfer
 from concourse.mybir import AluOpType, AxisListType, ActivationFunctionType
 
 W = 40
-WR = 8
+WF = 4
 ENG = 4
-NQ = 32
 CB = 4
 CRND = 100663296.0
 
 SCRATCH = {
     "L1": ("sbuf", [128, 4 * W], "bfloat16"),
+    "OWN": ("sbuf", [128, W], "bfloat16"),
+    "PR": ("sbuf", [128, 2 * W], "bfloat16"),
+    "ML1": ("sbuf", [128, 4 * WF], "float32"),
     "L2": ("sbuf", [128, 4 * W], "bfloat16"),
-    "NR": ("sbuf", [128, 4 * WR], "bfloat16"),
+    "NR": ("sbuf", [128, 4 * WF], "float32"),
     "ramp2": ("sbuf", [128, 128], "float32"),
     "ident": ("sbuf", [128, 128], "bfloat16"),
+    "dg1": ("sbuf", [128, 4 * 128], "bfloat16"),
     "dg": ("sbuf", [128, 4 * 128], "bfloat16"),
     "mlb": ("sbuf", [128, 12], "float32"),
-    "psb": ("psum", [128, 40], "float32"),
+    "ps1": ("psum", [128, 512], "float32"),
+    "psb": ("psum", [128, 512], "float32"),
     "e0": ("sbuf", [128, 4], "float32"),
-    "ownp": ("sbuf", [128, 36], "float32"),
-    "m4": ("sbuf", [128, 4], "float32"),
     "f4": ("sbuf", [128, 4], "float32"),
-    "pr": ("sbuf", [128, 4 * 36], "float32"),
-    "sm": ("sbuf", [128, 2 * 36], "float32"),
     "nrm": ("sbuf", [128, 4], "float32"),
     "w4": ("sbuf", [128, 4], "float32"),
     "rc": ("sbuf", [128, 4], "float32"),
     "ysb": ("sbuf", [128, 32], "bfloat16"),
 }
-SEMAPHORES = ["ld_o", "ld_ml", "cst", "ramp2", "ident", "pay1", "lcp", "e0", "own", "m40", "a1",
-              "sent", "negr", "m4", "f4", "p0", "p1", "p2", "p3", "s1", "s2", "pay2", "ar", "a2", "nrm", "w4",
+SEMAPHORES = ["ld_o", "ld_ml", "cst", "ramp2", "ident", "pay1", "e0", "own", "a1m", "a1o_1", "a1o_2", "a1o_3", "lc3",
+              "sent", "negr", "f4", "c0", "c1", "c2", "c3", "acc1", "pay2", "ar", "a2_1", "a2_2", "a2_3", "nrm", "w4",
               "rc", "d0", "d1", "d2", "d3", "acc", "y", "st"]
 
 
@@ -39,7 +39,7 @@ def rank_program(g, core, T, topo):
     V, A, PE, SY, S = g.vector, g.scalar, g.tensor, g.sync, T.sem
     ADD, SUB, MUL = AluOpType.add, AluOpType.subtract, AluOpType.mult
     EXP, COPY = ActivationFunctionType.Exp, ActivationFunctionType.Copy
-    L1, L2, NR, MLB = T.L1, T.L2, T.NR, T.mlb
+    L1, L2, NR, MLB, ML1, OWN, PR = T.L1, T.L2, T.NR, T.mlb, T.ML1, T.OWN, T.PR
 
     ranks = list(T.cores)
     here = [c for c in ranks if topo.host(c) == topo.host(core) and topo.chip(c) == topo.chip(core)]
@@ -48,7 +48,7 @@ def rank_program(g, core, T, topo):
     k = here.index(core)
     far1, far2 = (plane, cable) if k % 2 == 0 else (cable, plane)
 
-    def send(buf, w, c0, c1, dests, rsem):
+    def send(src, buf, w, c0, c1, dests, rsem):
         taken, trs = [], []
         for d, slot in sorted(dests, key=lambda x: topo.mask(core, x[0])):
             m = topo.mask(core, d)
@@ -56,81 +56,86 @@ def rank_program(g, core, T, topo):
             taken.extend(eng)
             rid, pid = topo.addr(d, core)
             trs.append(RemoteDMATransfer(dst_ids=[DstId(rid=rid, pnc=pid)], dma_engine_mask=sum(1 << e for e in eng),
-                                         remote_sem=rsem, src=buf[:, c0:c1], dst=buf[:, slot * w + c0:slot * w + c1]))
+                                         remote_sem=S[rsem % slot if "%" in rsem else rsem], src=src,
+                                         dst=buf[:, slot * w + c0:slot * w + c1]))
         g.remote_dma_fused(trs, local_sem=S.sent)
 
     for cb in range(CB):
         (SY if cb < CB // 2 else A).dma_start(MLB[cb:128:CB, 4:6], T.ml[:, :]).then_inc(S.ld_ml, 16)
     SY.dma_start(L1[:, 8:40], T.o[:, :]).then_inc(S.ld_o, 16)
+    g.iota(T.ramp2[:, :], [[-1, 128]], 0, 1, allow_small_or_imprecise_dtypes=True).then_inc(S.ramp2, 1)
     V.memset(MLB[:, 0:1], CRND).then_inc(S.cst, 1)
     V.memset(MLB[:, 8:9], 0.0).then_inc(S.cst, 1)
-    V.wait_ge(S.cst, 2)
-    V.wait_ge(S.ld_ml, 16 * CB)
-    V.tensor_tensor_scan(L1[:, 5:7], MLB[:, 4:12:4], MLB[:, 0:8:4], CRND, ADD, SUB).then_inc(S.pay1, 1)
-    A.wait_ge(S.ld_ml, 16 * CB)
-    A.activation(L1[:, 7:8], MLB[:, 5:6], COPY).then_inc(S.lcp, 1)
-
-    g.wait_ge(S.ld_o, 16)
-    g.wait_ge(S.lcp, 1)
-    g.wait_ge(S.pay1, 1)
-    send(L1, W, 5, 40, [(here[k ^ 2], 1), (far1[k], 2), (far1[k ^ 2], 3)], S.a1)
-    g.iota(T.ramp2[:, :], [[-1, 128]], 0, 1, allow_small_or_imprecise_dtypes=True).then_inc(S.ramp2, 1)
-
-    A.wait_ge(S.pay1, 1)
-    A.activation(T.e0[:, 0:1], L1[:, 6:7], EXP, scale=-1.0).then_inc(S.e0, 1)
-    A.wait_ge(S.e0, 1)
-    A.wait_ge(S.lcp, 1)
-    A.wait_ge(S.ld_o, 16)
-    A.activation(T.ownp[:, 0:33], L1[:, 7:40], COPY, scale=T.e0[:, 0:1]).then_inc(S.own, 1)
-    V.wait_ge(S.pay1, 1)
-    V.tensor_copy(T.m4[:, 0:1], L1[:, 5:6]).then_inc(S.m40, 1)
     V.wait_ge(S.ramp2, 1)
     V.tensor_scalar(T.ident[:, :], T.ramp2[:, :], 0.0, None, AluOpType.is_equal).then_inc(S.ident, 1)
 
-    V.wait_ge(S.a1, 3 * ENG)
-    V.tensor_reduce(NR[:, 0:1], L1[:, 5:4 * W:W], AxisListType.X, AluOpType.max, negate=True).then_inc(S.negr, 1)
-    V.tensor_tensor(T.m4[:, 1:4], L1[:, W + 5:4 * W:W], L1[:, W + 6:4 * W:W], SUB).then_inc(S.m4, 1)
+    to1 = [(here[k ^ 2], 1), (far1[k], 2), (far1[k ^ 2], 3)]
+    g.wait_ge(S.ld_ml, 16 * CB)
+    send(MLB[:, 4:6], ML1, WF, 0, 2, to1, "a1m")
+    g.wait_ge(S.ld_o, 16)
+    send(L1[:, 8:40], L1, W, 8, 40, to1, "a1o_%d")
+
+    V.wait_ge(S.cst, 2)
+    V.wait_ge(S.ld_ml, 16 * CB)
+    V.tensor_tensor_scan(ML1[:, 0:2], MLB[:, 4:12:4], MLB[:, 0:8:4], CRND, ADD, SUB).then_inc(S.pay1, 1)
+    A.wait_ge(S.pay1, 1)
+    A.activation(T.e0[:, 0:1], ML1[:, 1:2], EXP, scale=-1.0).then_inc(S.e0, 1)
+    A.wait_ge(S.e0, 1)
+    A.wait_ge(S.ld_ml, 16 * CB)
+    A.activation(OWN[:, 0:1], MLB[:, 5:6], COPY, scale=T.e0[:, 0:1]).then_inc(S.own, 1)
+    A.wait_ge(S.ld_o, 16)
+    A.activation(OWN[:, 1:33], L1[:, 8:40], COPY, scale=T.e0[:, 0:1]).then_inc(S.own, 1)
+
+    V.wait_ge(S.pay1, 1)
+    V.wait_ge(S.a1m, 3 * ENG)
+    V.tensor_reduce(NR[:, 0:1], ML1[:, 0:4 * WF:WF], AxisListType.X, AluOpType.max, negate=True).then_inc(S.negr, 1)
+    V.tensor_copy(L1[:, W + 7:4 * W:W], ML1[:, WF + 1:4 * WF:WF]).then_inc(S.lc3, 1)
 
     to2 = [(here[k ^ 1], 1), (far2[k], 2), (far2[k ^ 1], 3)]
     g.wait_ge(S.negr, 1)
-    send(NR, WR, 0, 1, to2, S.ar)
+    send(NR[:, 0:1], NR, WF, 0, 1, to2, "ar")
 
-    A.wait_ge(S.a1, 3 * ENG)
-    A.wait_ge(S.m40, 1)
+    A.wait_ge(S.a1m, 3 * ENG)
     A.wait_ge(S.negr, 1)
-    A.wait_ge(S.m4, 1)
-    A.activation(T.f4[:, 0:4], T.m4[:, 0:4], EXP, bias=NR[:, 0:1]).then_inc(S.f4, 1)
-    A.wait_ge(S.f4, 1)
-    for j in (1, 2, 3):
-        A.activation(T.pr[:, 36 * j:36 * j + 33], L1[:, W * j + 7:W * j + 40], COPY,
-                     scale=T.f4[:, j:j + 1]).then_inc(S["p%d" % j], 1)
+    A.activation(T.f4[:, 0:4], ML1[:, 0:4 * WF:WF], EXP, bias=NR[:, 0:1]).then_inc(S.f4, 1)
     V.wait_ge(S.f4, 1)
-    V.wait_ge(S.own, 1)
-    V.tensor_scalar(T.pr[:, 0:33], T.ownp[:, 0:33], T.f4[:, 0:1], None, MUL).then_inc(S.p0, 1)
-    V.wait_ge(S.p0, 1)
-    V.wait_ge(S.p1, 1)
-    V.tensor_tensor(T.sm[:, 0:33], T.pr[:, 0:33], T.pr[:, 36:69], ADD).then_inc(S.s1, 1)
-    V.wait_ge(S.s1, 1)
-    V.wait_ge(S.p2, 1)
-    V.tensor_tensor(T.sm[:, 36:69], T.sm[:, 0:33], T.pr[:, 72:105], ADD).then_inc(S.s2, 1)
-    V.wait_ge(S.s2, 1)
-    V.wait_ge(S.p3, 1)
-    V.tensor_tensor(L2[:, 7:40], T.sm[:, 36:69], T.pr[:, 108:141], ADD).then_inc(S.pay2, 1)
+    V.wait_ge(S.ident, 1)
+    for j in (2, 3):
+        V.tensor_scalar(T.dg1[:, j * 128:(j + 1) * 128], T.ident[:, :], T.f4[:, j:j + 1], None,
+                        MUL).then_inc(S["c%d" % j], 1)
+    A.wait_ge(S.f4, 1)
+    A.wait_ge(S.own, 2)
+    A.activation(PR[:, 0:33], OWN[:, 0:33], COPY, scale=T.f4[:, 0:1]).then_inc(S.c0, 1)
+    A.wait_ge(S.lc3, 1)
+    A.wait_ge(S.a1o_1, ENG)
+    A.activation(PR[:, W:W + 33], L1[:, W + 7:W + 40], COPY, scale=T.f4[:, 1:2]).then_inc(S.c1, 1)
+    PE.wait_ge(S.ident, 1)
+    PE.wait_ge(S.c0, 1)
+    PE.matmul(T.ps1[:, 0:33], T.ident[:, :], PR[:, 0:33], True, False)
+    PE.wait_ge(S.c1, 1)
+    PE.matmul(T.ps1[:, 0:33], T.ident[:, :], PR[:, W:W + 33], False, False)
+    PE.wait_ge(S.lc3, 1)
+    for j in (2, 3):
+        PE.wait_ge(S["c%d" % j], 1)
+        PE.wait_ge(S["a1o_%d" % j], ENG)
+        mm = PE.matmul(T.ps1[:, 0:33], T.dg1[:, j * 128:(j + 1) * 128], L1[:, W * j + 7:W * j + 40], False, j == 3)
+    mm.then_inc(S.acc1, 1)
+    V.wait_ge(S.acc1, 1)
+    V.tensor_copy(L2[:, 7:40], T.ps1[:, 0:33]).then_inc(S.pay2, 1)
 
     g.wait_ge(S.pay2, 1)
-    send(L2, W, 7, 40, to2, S.a2)
+    send(L2[:, 7:40], L2, W, 7, 40, to2, "a2_%d")
 
     V.wait_ge(S.negr, 1)
     V.wait_ge(S.ar, 3 * ENG)
-    V.tensor_reduce(T.nrm[:, 0:1], NR[:, 0:4 * WR:WR], AxisListType.X, AluOpType.min).then_inc(S.nrm, 1)
+    V.tensor_reduce(T.nrm[:, 0:1], NR[:, 0:4 * WF:WF], AxisListType.X, AluOpType.min).then_inc(S.nrm, 1)
     A.wait_ge(S.ar, 3 * ENG)
     A.wait_ge(S.nrm, 1)
-    A.activation(T.w4[:, 0:4], NR[:, 0:4 * WR:WR], EXP, bias=T.nrm[:, 0:1], scale=-1.0).then_inc(S.w4, 1)
+    A.activation(T.w4[:, 0:4], NR[:, 0:4 * WF:WF], EXP, bias=T.nrm[:, 0:1], scale=-1.0).then_inc(S.w4, 1)
     A.wait_ge(S.w4, 1)
     A.wait_ge(S.ident, 1)
     A.activation(T.dg[:, 3 * 128:4 * 128], T.ident[:, :], COPY, scale=T.w4[:, 3:4]).then_inc(S.d3, 1)
     V.wait_ge(S.w4, 1)
-    V.wait_ge(S.ident, 1)
     for j in (0, 1, 2):
         V.tensor_scalar(T.dg[:, j * 128:(j + 1) * 128], T.ident[:, :], T.w4[:, j:j + 1], None,
                         MUL).then_inc(S["d%d" % j], 1)
@@ -138,8 +143,8 @@ def rank_program(g, core, T, topo):
     PE.wait_ge(S.pay2, 1)
     for j in range(4):
         PE.wait_ge(S["d%d" % j], 1)
-        if j == 1:
-            PE.wait_ge(S.a2, 3 * ENG)
+        if j:
+            PE.wait_ge(S["a2_%d" % j], ENG)
         mm = PE.matmul(T.psb[:, 0:33], T.dg[:, j * 128:(j + 1) * 128], L2[:, W * j + 7:W * j + 40], j == 0, j == 3)
     mm.then_inc(S.acc, 1)
     V.wait_ge(S.acc, 1)
@@ -150,4 +155,4 @@ def rank_program(g, core, T, topo):
     SY.wait_ge(S.y, 1)
     SY.dma_start(T.y[:, :], T.ysb[:, :]).then_inc(S.st, 16)
     SY.wait_ge(S.st, 16)
-    g.wait_ge(S.sent, 9 * ENG)
+    g.wait_ge(S.sent, 12 * ENG)

@@ -1,8 +1,9 @@
 from concourse.bass import DstId, RemoteDMATransfer
 from concourse.mybir import AluOpType, AxisListType, ActivationFunctionType
 
-W = 40
-WF = 4
+W = 32
+PW = 12
+NE = PW // 2
 ENG = 4
 CB = 4
 CRND = 100663296.0
@@ -11,35 +12,37 @@ SCRATCH = {
     "L1": ("sbuf", [128, 4 * W], "bfloat16"),
     "OWN": ("sbuf", [128, W], "bfloat16"),
     "PR": ("sbuf", [128, 2 * W], "bfloat16"),
-    "ML1": ("sbuf", [128, 4 * WF], "float32"),
+    "PR2": ("sbuf", [128, 2 * W], "bfloat16"),
+    "SC": ("sbuf", [128, 4 * PW], "float32"),
     "L2": ("sbuf", [128, 4 * W], "bfloat16"),
-    "NR": ("sbuf", [128, 4 * WF], "float32"),
     "ramp2": ("sbuf", [128, 128], "float32"),
     "ident": ("sbuf", [128, 128], "bfloat16"),
-    "dg1": ("sbuf", [128, 4 * 128], "bfloat16"),
-    "dg": ("sbuf", [128, 4 * 128], "bfloat16"),
-    "mlb": ("sbuf", [128, 12], "float32"),
+    "dg1": ("sbuf", [128, 2 * 128], "bfloat16"),
+    "dg": ("sbuf", [128, 2 * 128], "bfloat16"),
     "ps1": ("psum", [128, 512], "float32"),
     "psb": ("psum", [128, 512], "float32"),
     "e0": ("sbuf", [128, 4], "float32"),
+    "nr": ("sbuf", [128, 4], "float32"),
     "f4": ("sbuf", [128, 4], "float32"),
-    "nrm": ("sbuf", [128, 4], "float32"),
-    "w4": ("sbuf", [128, 4], "float32"),
+    "nm": ("sbuf", [128, 4], "float32"),
+    "E": ("sbuf", [128, 4 * NE], "float32"),
+    "El": ("sbuf", [128, 4 * NE], "float32"),
+    "D": ("sbuf", [128, 4], "float32"),
     "rc": ("sbuf", [128, 4], "float32"),
     "ysb": ("sbuf", [128, 32], "bfloat16"),
 }
-SEMAPHORES = ["ld_o", "ld_ml", "cst", "ramp2", "ident", "pay1", "e0", "own", "a1m", "a1o_1", "a1o_2", "a1o_3", "lc3",
-              "sent", "negr", "f4", "c0", "c1", "c2", "c3", "acc1", "pay2", "ar", "a2_1", "a2_2", "a2_3", "nrm", "w4",
-              "rc", "d0", "d1", "d2", "d3", "acc", "y", "st"]
+SEMAPHORES = ["ld_o", "ld_ml", "cst", "ramp2", "ident", "hi", "e0", "own", "a1m", "a1o_1", "a1o_2", "a1o_3",
+              "sent", "rpos", "negr", "f4", "c0", "c1", "c2", "c3", "acc1", "pay2", "ar", "a2_1", "a2_2", "a2_3", "nm",
+              "E", "El", "D", "rc", "d0", "d1", "d2", "d3", "acc", "y", "st"]
 
 
 def rank_program(g, core, T, topo):
     if T.rank_of(core) is None:
         return
     V, A, PE, SY, S = g.vector, g.scalar, g.tensor, g.sync, T.sem
-    ADD, SUB, MUL = AluOpType.add, AluOpType.subtract, AluOpType.mult
+    ADD, SUB, MUL, MAX = AluOpType.add, AluOpType.subtract, AluOpType.mult, AluOpType.max
     EXP, COPY = ActivationFunctionType.Exp, ActivationFunctionType.Copy
-    L1, L2, NR, MLB, ML1, OWN, PR = T.L1, T.L2, T.NR, T.mlb, T.ML1, T.OWN, T.PR
+    L1, L2, SC, OWN, PR, PR2 = T.L1, T.L2, T.SC, T.OWN, T.PR, T.PR2
 
     ranks = list(T.cores)
     here = [c for c in ranks if topo.host(c) == topo.host(core) and topo.chip(c) == topo.chip(core)]
@@ -48,7 +51,7 @@ def rank_program(g, core, T, topo):
     k = here.index(core)
     far1, far2 = (plane, cable) if k % 2 == 0 else (cable, plane)
 
-    def send(src, buf, w, c0, c1, dests, rsem):
+    def send(src, buf, w, dests, rsem):
         taken, trs = [], []
         for d, slot in sorted(dests, key=lambda x: topo.mask(core, x[0])):
             m = topo.mask(core, d)
@@ -57,100 +60,113 @@ def rank_program(g, core, T, topo):
             rid, pid = topo.addr(d, core)
             trs.append(RemoteDMATransfer(dst_ids=[DstId(rid=rid, pnc=pid)], dma_engine_mask=sum(1 << e for e in eng),
                                          remote_sem=S[rsem % slot if "%" in rsem else rsem], src=src,
-                                         dst=buf[:, slot * w + c0:slot * w + c1]))
+                                         dst=buf[:, slot * w:(slot + 1) * w]))
         g.remote_dma_fused(trs, local_sem=S.sent)
 
     for cb in range(CB):
-        (SY if cb < CB // 2 else A).dma_start(MLB[cb:128:CB, 4:6], T.ml[:, :]).then_inc(S.ld_ml, 16)
-    SY.dma_start(L1[:, 8:40], T.o[:, :]).then_inc(S.ld_o, 16)
+        (SY if cb < CB // 2 else A).dma_start(SC[cb:128:CB, 0:2], T.ml[:, :]).then_inc(S.ld_ml, 16)
+    SY.dma_start(L1[:, 0:W], T.o[:, :]).then_inc(S.ld_o, 16)
     g.iota(T.ramp2[:, :], [[-1, 128]], 0, 1, allow_small_or_imprecise_dtypes=True).then_inc(S.ramp2, 1)
-    V.memset(MLB[:, 0:1], CRND).then_inc(S.cst, 1)
-    V.memset(MLB[:, 8:9], 0.0).then_inc(S.cst, 1)
+    V.memset(SC[:, 9:12:2], 0.0).then_inc(S.cst, 1)
     V.wait_ge(S.ramp2, 1)
     V.tensor_scalar(T.ident[:, :], T.ramp2[:, :], 0.0, None, AluOpType.is_equal).then_inc(S.ident, 1)
 
     to1 = [(here[k ^ 2], 1), (far1[k], 2), (far1[k ^ 2], 3)]
     g.wait_ge(S.ld_ml, 16 * CB)
-    send(MLB[:, 4:6], ML1, WF, 0, 2, to1, "a1m")
+    send(SC[:, 0:2], SC, 2, to1, "a1m")
     g.wait_ge(S.ld_o, 16)
-    send(L1[:, 8:40], L1, W, 8, 40, to1, "a1o_%d")
+    send(L1[:, 0:W], L1, W, to1, "a1o_%d")
 
-    V.wait_ge(S.cst, 2)
     V.wait_ge(S.ld_ml, 16 * CB)
-    V.tensor_tensor_scan(ML1[:, 0:2], MLB[:, 4:12:4], MLB[:, 0:8:4], CRND, ADD, SUB).then_inc(S.pay1, 1)
-    A.wait_ge(S.pay1, 1)
-    A.activation(T.e0[:, 0:1], ML1[:, 1:2], EXP, scale=-1.0).then_inc(S.e0, 1)
-    A.wait_ge(S.e0, 1)
+    V.tensor_scalar(SC[:, 8:9], SC[:, 0:1], CRND, CRND, ADD, SUB).then_inc(S.hi, 1)
+    A.wait_ge(S.hi, 1)
     A.wait_ge(S.ld_ml, 16 * CB)
-    A.activation(OWN[:, 0:1], MLB[:, 5:6], COPY, scale=T.e0[:, 0:1]).then_inc(S.own, 1)
+    A.activation(T.e0[:, 0:1], SC[:, 8:9], EXP, bias=SC[:, 0:1], scale=-1.0).then_inc(S.e0, 1)
+    A.wait_ge(S.e0, 1)
     A.wait_ge(S.ld_o, 16)
-    A.activation(OWN[:, 1:33], L1[:, 8:40], COPY, scale=T.e0[:, 0:1]).then_inc(S.own, 1)
+    A.activation(OWN[:, 0:W], L1[:, 0:W], COPY, scale=T.e0[:, 0:1]).then_inc(S.own, 1)
 
-    V.wait_ge(S.pay1, 1)
     V.wait_ge(S.a1m, 3 * ENG)
-    V.tensor_reduce(NR[:, 0:1], ML1[:, 0:4 * WF:WF], AxisListType.X, AluOpType.max, negate=True).then_inc(S.negr, 1)
-    V.tensor_copy(L1[:, W + 7:4 * W:W], ML1[:, WF + 1:4 * WF:WF]).then_inc(S.lc3, 1)
+    V.tensor_reduce(SC[:, 10:11], SC[:, 0:8:2], AxisListType.X, MAX).then_inc(S.rpos, 1)
+    V.tensor_reduce(T.nr[:, 0:1], SC[:, 0:8:2], AxisListType.X, MAX, negate=True).then_inc(S.negr, 1)
 
     to2 = [(here[k ^ 1], 1), (far2[k], 2), (far2[k ^ 1], 3)]
-    g.wait_ge(S.negr, 1)
-    send(NR[:, 0:1], NR, WF, 0, 1, to2, "ar")
+    g.wait_ge(S.a1m, 3 * ENG)
+    g.wait_ge(S.cst, 1)
+    g.wait_ge(S.hi, 1)
+    g.wait_ge(S.rpos, 1)
+    send(SC[:, 0:PW], SC, PW, to2, "ar")
 
     A.wait_ge(S.a1m, 3 * ENG)
     A.wait_ge(S.negr, 1)
-    A.activation(T.f4[:, 0:4], ML1[:, 0:4 * WF:WF], EXP, bias=NR[:, 0:1]).then_inc(S.f4, 1)
+    A.activation(T.f4[:, 0:4], SC[:, 2:10:2], EXP, bias=T.nr[:, 0:1]).then_inc(S.f4, 1)
     V.wait_ge(S.f4, 1)
     V.wait_ge(S.ident, 1)
     for j in (2, 3):
-        V.tensor_scalar(T.dg1[:, j * 128:(j + 1) * 128], T.ident[:, :], T.f4[:, j:j + 1], None,
+        V.tensor_scalar(T.dg1[:, (j - 2) * 128:(j - 1) * 128], T.ident[:, :], T.f4[:, j - 1:j], None,
                         MUL).then_inc(S["c%d" % j], 1)
     A.wait_ge(S.f4, 1)
-    A.wait_ge(S.own, 2)
-    A.activation(PR[:, 0:33], OWN[:, 0:33], COPY, scale=T.f4[:, 0:1]).then_inc(S.c0, 1)
-    A.wait_ge(S.lc3, 1)
+    A.wait_ge(S.own, 1)
+    A.activation(PR[:, 0:W], OWN[:, 0:W], COPY, scale=T.f4[:, 3:4]).then_inc(S.c0, 1)
     A.wait_ge(S.a1o_1, ENG)
-    A.activation(PR[:, W:W + 33], L1[:, W + 7:W + 40], COPY, scale=T.f4[:, 1:2]).then_inc(S.c1, 1)
+    A.activation(PR[:, W:2 * W], L1[:, W:2 * W], COPY, scale=T.f4[:, 0:1]).then_inc(S.c1, 1)
     PE.wait_ge(S.ident, 1)
     PE.wait_ge(S.c0, 1)
-    PE.matmul(T.ps1[:, 0:33], T.ident[:, :], PR[:, 0:33], True, False)
+    PE.matmul(T.ps1[:, 0:W], T.ident[:, :], PR[:, 0:W], True, False)
     PE.wait_ge(S.c1, 1)
-    PE.matmul(T.ps1[:, 0:33], T.ident[:, :], PR[:, W:W + 33], False, False)
-    PE.wait_ge(S.lc3, 1)
+    PE.matmul(T.ps1[:, 0:W], T.ident[:, :], PR[:, W:2 * W], False, False)
     for j in (2, 3):
         PE.wait_ge(S["c%d" % j], 1)
         PE.wait_ge(S["a1o_%d" % j], ENG)
-        mm = PE.matmul(T.ps1[:, 0:33], T.dg1[:, j * 128:(j + 1) * 128], L1[:, W * j + 7:W * j + 40], False, j == 3)
+        mm = PE.matmul(T.ps1[:, 0:W], T.dg1[:, (j - 2) * 128:(j - 1) * 128], L1[:, W * j:W * (j + 1)], False, j == 3)
     mm.then_inc(S.acc1, 1)
     V.wait_ge(S.acc1, 1)
-    V.tensor_copy(L2[:, 7:40], T.ps1[:, 0:33]).then_inc(S.pay2, 1)
+    V.tensor_copy(L2[:, 0:W], T.ps1[:, 0:W]).then_inc(S.pay2, 1)
 
     g.wait_ge(S.pay2, 1)
-    send(L2[:, 7:40], L2, W, 7, 40, to2, "a2_%d")
+    send(L2[:, 0:W], L2, W, to2, "a2_%d")
 
-    V.wait_ge(S.negr, 1)
+    V.wait_ge(S.cst, 1)
+    V.wait_ge(S.hi, 1)
+    V.wait_ge(S.rpos, 1)
     V.wait_ge(S.ar, 3 * ENG)
-    V.tensor_reduce(T.nrm[:, 0:1], NR[:, 0:4 * WF:WF], AxisListType.X, AluOpType.min).then_inc(S.nrm, 1)
+    V.tensor_reduce(T.nm[:, 0:1], SC[:, 0:4 * PW:2], AxisListType.X, MAX, negate=True).then_inc(S.nm, 1)
+    A.wait_ge(S.cst, 1)
+    A.wait_ge(S.rpos, 1)
     A.wait_ge(S.ar, 3 * ENG)
-    A.wait_ge(S.nrm, 1)
-    A.activation(T.w4[:, 0:4], NR[:, 0:4 * WF:WF], EXP, bias=T.nrm[:, 0:1], scale=-1.0).then_inc(S.w4, 1)
-    A.wait_ge(S.w4, 1)
-    A.wait_ge(S.ident, 1)
-    A.activation(T.dg[:, 3 * 128:4 * 128], T.ident[:, :], COPY, scale=T.w4[:, 3:4]).then_inc(S.d3, 1)
-    V.wait_ge(S.w4, 1)
-    for j in (0, 1, 2):
-        V.tensor_scalar(T.dg[:, j * 128:(j + 1) * 128], T.ident[:, :], T.w4[:, j:j + 1], None,
-                        MUL).then_inc(S["d%d" % j], 1)
+    A.wait_ge(S.nm, 1)
+    A.activation(T.E[:, :], SC[:, 0:4 * PW:2], EXP, bias=T.nm[:, 0:1]).then_inc(S.E, 1)
 
-    PE.wait_ge(S.pay2, 1)
-    for j in range(4):
+    def w(j):
+        return T.E[:, NE * j + NE - 1:NE * j + NE]
+
+    V.wait_ge(S.E, 1)
+    V.tensor_tensor(T.El[:, :], T.E[:, :], SC[:, 1:4 * PW:2], MUL).then_inc(S.El, 1)
+    V.tensor_scalar(T.dg[:, 0:128], T.ident[:, :], w(2), None, MUL).then_inc(S.d2, 1)
+    V.wait_ge(S.El, 1)
+    V.tensor_reduce(T.D[:, 0:1], T.El[:, :], AxisListType.X, ADD).then_inc(S.D, 1)
+    V.wait_ge(S.D, 1)
+    V.reciprocal(T.rc[:, 0:1], T.D[:, 0:1]).then_inc(S.rc, 1)
+    A.wait_ge(S.E, 1)
+    A.wait_ge(S.pay2, 1)
+    A.activation(PR2[:, 0:W], L2[:, 0:W], COPY, scale=w(0)).then_inc(S.d0, 1)
+    A.wait_ge(S.ident, 1)
+    A.activation(T.dg[:, 128:256], T.ident[:, :], COPY, scale=w(3)).then_inc(S.d3, 1)
+    A.wait_ge(S.a2_1, ENG)
+    A.activation(PR2[:, W:2 * W], L2[:, W:2 * W], COPY, scale=w(1)).then_inc(S.d1, 1)
+
+    PE.wait_ge(S.d0, 1)
+    PE.matmul(T.psb[:, 0:W], T.ident[:, :], PR2[:, 0:W], True, False)
+    PE.wait_ge(S.d1, 1)
+    PE.matmul(T.psb[:, 0:W], T.ident[:, :], PR2[:, W:2 * W], False, False)
+    for j in (2, 3):
         PE.wait_ge(S["d%d" % j], 1)
-        if j:
-            PE.wait_ge(S["a2_%d" % j], ENG)
-        mm = PE.matmul(T.psb[:, 0:33], T.dg[:, j * 128:(j + 1) * 128], L2[:, W * j + 7:W * j + 40], j == 0, j == 3)
+        PE.wait_ge(S["a2_%d" % j], ENG)
+        mm = PE.matmul(T.psb[:, 0:W], T.dg[:, (j - 2) * 128:(j - 1) * 128], L2[:, W * j:W * (j + 1)], False, j == 3)
     mm.then_inc(S.acc, 1)
-    V.wait_ge(S.acc, 1)
-    V.reciprocal(T.rc[:, 0:1], T.psb[:, 0:1]).then_inc(S.rc, 1)
     V.wait_ge(S.rc, 1)
-    V.tensor_scalar(T.ysb[:, :], T.psb[:, 1:33], T.rc[:, 0:1], None, MUL).then_inc(S.y, 1)
+    V.wait_ge(S.acc, 1)
+    V.tensor_scalar(T.ysb[:, :], T.psb[:, 0:W], T.rc[:, 0:1], None, MUL).then_inc(S.y, 1)
 
     SY.wait_ge(S.y, 1)
     SY.dma_start(T.y[:, :], T.ysb[:, :]).then_inc(S.st, 16)

from concourse.bass import DstId, RemoteDMATransfer
from concourse.mybir import AluOpType, AxisListType, ActivationFunctionType

W = 32
PW = 12
NE = PW // 2
ENG = 4
CB = 4
CRND = 100663296.0

SCRATCH = {
    "L1": ("sbuf", [128, 4 * W], "bfloat16"),
    "OWN": ("sbuf", [128, W], "bfloat16"),
    "PR": ("sbuf", [128, 2 * W], "bfloat16"),
    "PR2": ("sbuf", [128, 2 * W], "bfloat16"),
    "SC": ("sbuf", [128, 4 * PW], "float32"),
    "L2": ("sbuf", [128, 4 * W], "bfloat16"),
    "ramp2": ("sbuf", [128, 128], "float32"),
    "ident": ("sbuf", [128, 128], "bfloat16"),
    "dg1": ("sbuf", [128, 2 * 128], "bfloat16"),
    "dg": ("sbuf", [128, 2 * 128], "bfloat16"),
    "ps1": ("psum", [128, 512], "float32"),
    "psb": ("psum", [128, 512], "float32"),
    "e0": ("sbuf", [128, 4], "float32"),
    "nr": ("sbuf", [128, 4], "float32"),
    "f4": ("sbuf", [128, 4], "float32"),
    "nm": ("sbuf", [128, 4], "float32"),
    "E": ("sbuf", [128, 4 * NE], "float32"),
    "El": ("sbuf", [128, 4 * NE], "float32"),
    "D": ("sbuf", [128, 4], "float32"),
    "rc": ("sbuf", [128, 4], "float32"),
    "ysb": ("sbuf", [128, 32], "bfloat16"),
}
SEMAPHORES = ["ld_o", "ld_ml", "cst", "ramp2", "ident", "hi", "e0", "own", "a1m", "a1o_1", "a1o_2", "a1o_3",
              "sent", "rpos", "negr", "f4", "c0", "c1", "c2", "c3", "acc1", "pay2", "ar", "a2_1", "a2_2", "a2_3", "nm",
              "E", "El", "D", "rc", "d0", "d1", "d2", "d3", "acc", "y", "st"]


def rank_program(g, core, T, topo):
    if T.rank_of(core) is None:
        return
    V, A, PE, SY, S = g.vector, g.scalar, g.tensor, g.sync, T.sem
    ADD, SUB, MUL, MAX = AluOpType.add, AluOpType.subtract, AluOpType.mult, AluOpType.max
    EXP, COPY = ActivationFunctionType.Exp, ActivationFunctionType.Copy
    L1, L2, SC, OWN, PR, PR2 = T.L1, T.L2, T.SC, T.OWN, T.PR, T.PR2

    ranks = list(T.cores)
    here = [c for c in ranks if topo.host(c) == topo.host(core) and topo.chip(c) == topo.chip(core)]
    plane = [c for c in ranks if topo.same_plane(core, c)]
    cable = [c for c in ranks if topo.rack(topo.host(c)) != topo.rack(topo.host(core)) and topo.may_write(core, c)]
    k = here.index(core)
    far1, far2 = (plane, cable) if k % 2 == 0 else (cable, plane)

    def send(src, buf, w, dests, rsem):
        taken, trs = [], []
        for d, slot in sorted(dests, key=lambda x: topo.mask(core, x[0])):
            m = topo.mask(core, d)
            eng = [e for e in range(m.bit_length()) if (m >> e) & 1 and e not in taken][:ENG]
            taken.extend(eng)
            rid, pid = topo.addr(d, core)
            trs.append(RemoteDMATransfer(dst_ids=[DstId(rid=rid, pnc=pid)], dma_engine_mask=sum(1 << e for e in eng),
                                         remote_sem=S[rsem % slot if "%" in rsem else rsem], src=src,
                                         dst=buf[:, slot * w:(slot + 1) * w]))
        g.remote_dma_fused(trs, local_sem=S.sent)

    for cb in range(CB):
        (SY if cb < CB // 2 else A).dma_start(SC[cb:128:CB, 0:2], T.ml[:, :]).then_inc(S.ld_ml, 16)
    SY.dma_start(L1[:, 0:W], T.o[:, :]).then_inc(S.ld_o, 16)
    g.iota(T.ramp2[:, :], [[-1, 128]], 0, 1, allow_small_or_imprecise_dtypes=True).then_inc(S.ramp2, 1)
    V.memset(SC[:, 9:12:2], 0.0).then_inc(S.cst, 1)
    V.wait_ge(S.ramp2, 1)
    V.tensor_scalar(T.ident[:, :], T.ramp2[:, :], 0.0, None, AluOpType.is_equal).then_inc(S.ident, 1)

    to1 = [(here[k ^ 2], 1), (far1[k], 2), (far1[k ^ 2], 3)]
    g.wait_ge(S.ld_ml, 16 * CB)
    send(SC[:, 0:2], SC, 2, to1, "a1m")
    g.wait_ge(S.ld_o, 16)
    send(L1[:, 0:W], L1, W, to1, "a1o_%d")

    V.wait_ge(S.ld_ml, 16 * CB)
    V.tensor_scalar(SC[:, 8:9], SC[:, 0:1], CRND, CRND, ADD, SUB).then_inc(S.hi, 1)
    A.wait_ge(S.hi, 1)
    A.wait_ge(S.ld_ml, 16 * CB)
    A.activation(T.e0[:, 0:1], SC[:, 8:9], EXP, bias=SC[:, 0:1], scale=-1.0).then_inc(S.e0, 1)
    A.wait_ge(S.e0, 1)
    A.wait_ge(S.ld_o, 16)
    A.activation(OWN[:, 0:W], L1[:, 0:W], COPY, scale=T.e0[:, 0:1]).then_inc(S.own, 1)

    V.wait_ge(S.a1m, 3 * ENG)
    V.tensor_reduce(SC[:, 10:11], SC[:, 0:8:2], AxisListType.X, MAX).then_inc(S.rpos, 1)
    V.tensor_reduce(T.nr[:, 0:1], SC[:, 0:8:2], AxisListType.X, MAX, negate=True).then_inc(S.negr, 1)

    to2 = [(here[k ^ 1], 1), (far2[k], 2), (far2[k ^ 1], 3)]
    g.wait_ge(S.a1m, 3 * ENG)
    g.wait_ge(S.cst, 1)
    g.wait_ge(S.hi, 1)
    g.wait_ge(S.rpos, 1)
    send(SC[:, 0:PW], SC, PW, to2, "ar")

    A.wait_ge(S.a1m, 3 * ENG)
    A.wait_ge(S.negr, 1)
    A.activation(T.f4[:, 0:4], SC[:, 2:10:2], EXP, bias=T.nr[:, 0:1]).then_inc(S.f4, 1)
    V.wait_ge(S.f4, 1)
    V.wait_ge(S.ident, 1)
    for j in (2, 3):
        V.tensor_scalar(T.dg1[:, (j - 2) * 128:(j - 1) * 128], T.ident[:, :], T.f4[:, j - 1:j], None,
                        MUL).then_inc(S["c%d" % j], 1)
    A.wait_ge(S.f4, 1)
    A.wait_ge(S.own, 1)
    A.activation(PR[:, 0:W], OWN[:, 0:W], COPY, scale=T.f4[:, 3:4]).then_inc(S.c0, 1)
    A.wait_ge(S.a1o_1, ENG)
    A.activation(PR[:, W:2 * W], L1[:, W:2 * W], COPY, scale=T.f4[:, 0:1]).then_inc(S.c1, 1)
    PE.wait_ge(S.ident, 1)
    PE.wait_ge(S.c0, 1)
    PE.matmul(T.ps1[:, 0:W], T.ident[:, :], PR[:, 0:W], True, False)
    PE.wait_ge(S.c1, 1)
    PE.matmul(T.ps1[:, 0:W], T.ident[:, :], PR[:, W:2 * W], False, False)
    for j in (2, 3):
        PE.wait_ge(S["c%d" % j], 1)
        PE.wait_ge(S["a1o_%d" % j], ENG)
        mm = PE.matmul(T.ps1[:, 0:W], T.dg1[:, (j - 2) * 128:(j - 1) * 128], L1[:, W * j:W * (j + 1)], False, j == 3)
    mm.then_inc(S.acc1, 1)
    V.wait_ge(S.acc1, 1)
    V.tensor_copy(L2[:, 0:W], T.ps1[:, 0:W]).then_inc(S.pay2, 1)

    g.wait_ge(S.pay2, 1)
    send(L2[:, 0:W], L2, W, to2, "a2_%d")

    V.wait_ge(S.cst, 1)
    V.wait_ge(S.hi, 1)
    V.wait_ge(S.rpos, 1)
    V.wait_ge(S.ar, 3 * ENG)
    V.tensor_reduce(T.nm[:, 0:1], SC[:, 0:4 * PW:2], AxisListType.X, MAX, negate=True).then_inc(S.nm, 1)
    A.wait_ge(S.cst, 1)
    A.wait_ge(S.rpos, 1)
    A.wait_ge(S.ar, 3 * ENG)
    A.wait_ge(S.nm, 1)
    A.activation(T.E[:, :], SC[:, 0:4 * PW:2], EXP, bias=T.nm[:, 0:1]).then_inc(S.E, 1)

    def w(j):
        return T.E[:, NE * j + NE - 1:NE * j + NE]

    V.wait_ge(S.E, 1)
    V.tensor_tensor(T.El[:, :], T.E[:, :], SC[:, 1:4 * PW:2], MUL).then_inc(S.El, 1)
    V.tensor_scalar(T.dg[:, 0:128], T.ident[:, :], w(2), None, MUL).then_inc(S.d2, 1)
    V.wait_ge(S.El, 1)
    V.tensor_reduce(T.D[:, 0:1], T.El[:, :], AxisListType.X, ADD).then_inc(S.D, 1)
    V.wait_ge(S.D, 1)
    V.reciprocal(T.rc[:, 0:1], T.D[:, 0:1]).then_inc(S.rc, 1)
    A.wait_ge(S.E, 1)
    A.wait_ge(S.pay2, 1)
    A.activation(PR2[:, 0:W], L2[:, 0:W], COPY, scale=w(0)).then_inc(S.d0, 1)
    A.wait_ge(S.ident, 1)
    A.activation(T.dg[:, 128:256], T.ident[:, :], COPY, scale=w(3)).then_inc(S.d3, 1)
    A.wait_ge(S.a2_1, ENG)
    A.activation(PR2[:, W:2 * W], L2[:, W:2 * W], COPY, scale=w(1)).then_inc(S.d1, 1)

    PE.wait_ge(S.d0, 1)
    PE.matmul(T.psb[:, 0:W], T.ident[:, :], PR2[:, 0:W], True, False)
    PE.wait_ge(S.d1, 1)
    PE.matmul(T.psb[:, 0:W], T.ident[:, :], PR2[:, W:2 * W], False, False)
    for j in (2, 3):
        PE.wait_ge(S["d%d" % j], 1)
        PE.wait_ge(S["a2_%d" % j], ENG)
        mm = PE.matmul(T.psb[:, 0:W], T.dg[:, (j - 2) * 128:(j - 1) * 128], L2[:, W * j:W * (j + 1)], False, j == 3)
    mm.then_inc(S.acc, 1)
    V.wait_ge(S.rc, 1)
    V.wait_ge(S.acc, 1)
    V.tensor_scalar(T.ysb[:, :], T.psb[:, 0:W], T.rc[:, 0:1], None, MUL).then_inc(S.y, 1)

    SY.wait_ge(S.y, 1)
    SY.dma_start(T.y[:, :], T.ysb[:, :]).then_inc(S.st, 16)
    SY.wait_ge(S.st, 16)
    g.wait_ge(S.sent, 12 * ENG)
